import numpy as np
import ml_dtypes

BF16 = ml_dtypes.bfloat16


def bf(x):
    return np.asarray(x, np.float32).astype(BF16)


def f32(x):
    return np.asarray(x, np.float32)


def f64(x):
    return np.asarray(x).astype(np.float64)


def striped(idx):
    return np.concatenate([l.reshape(-1, 16).T for l in idx])


def rows(idx, k):
    return np.tile(np.repeat(idx, 16, axis=0), (k // (16 * 8), 1))


def look(tab, idx):
    return np.take_along_axis(f64(tab), rows(idx, len(tab)), axis=1)


K, S, D, V, N, M = 512, 2048, 3, 512, 1536, 512


def setup_inputs():
    return {"tab": f32(np.random.standard_normal((K, S))), "x0": f32(np.random.standard_normal((K, V))), "w": bf(np.random.standard_normal((K, M)) / np.sqrt(K)), "b": f32(0.5 * np.random.standard_normal((M, 1))), "offs": striped(np.stack([np.random.permutation(S)[:N] for _ in range(8)]))}


def reference(tab, x0, w, b, offs):
    idx = np.stack([g.T.reshape(-1) for g in np.split(offs, 8)])
    x = f64(x0)
    for d in range(D):
        x = np.maximum(x, look(tab, idx[:, d * V:(d + 1) * V]))
    y = f64(w).T @ x
    return np.maximum(y + f64(b), 0.0)

@@ -1,0 +1,62 @@
+import concourse.mybir as mybir
+
+P = 128
+ROWS, TABLE_COLS = 512, 2048
+NEIGHBOURS, POOLED = 3, 512
+OUT_ROWS = 512
+BLOCKS = ROWS // P
+OUT_BLOCKS = OUT_ROWS // P
+PIECE = POOLED // 16
+
+F32, BF16, U16 = mybir.dt.float32, mybir.dt.bfloat16, mybir.dt.uint16
+ADD, MAX = mybir.AluOpType.add, mybir.AluOpType.max
+RELU = mybir.ActivationFunctionType.Relu
+
+FLOPS = 2 * ROWS * OUT_ROWS * POOLED
+
+
+def tile_lookup_pool_max_relu_kernel(tc, tab, x0, w, b, offs, out):
+    nc = tc.nc
+    with (
+        tc.tile_pool(name="held", bufs=1) as held,
+        tc.psum_pool(name="psum", bufs=1) as psum,
+    ):
+        offsets = held.tile([P, NEIGHBOURS * PIECE], U16, name="offsets")
+        nc.sync.dma_start(offsets[:], offs)
+
+        windows, centres = [], []
+        weights = held.tile([P, BLOCKS, OUT_ROWS], BF16, name="weights")
+        bias = held.tile([P, OUT_BLOCKS], F32, name="bias")
+        for k in range(BLOCKS):
+            rows = slice(k * P, (k + 1) * P)
+            window = held.tile([P, TABLE_COLS], F32, name=f"window{k}")
+            centre = held.tile([P, POOLED], F32, name=f"centre{k}")
+            nc.sync.dma_start(centre[:], x0[rows, :])
+            nc.sync.dma_start(window[:], tab[rows, :])
+            windows.append(window)
+            centres.append(centre)
+            if k == 1:
+                nc.sync.dma_start(weights[:], w.rearrange("(k p) m -> p k m", p=P))
+                nc.sync.dma_start(bias[:], b.rearrange("(t p) one -> p (t one)", p=P))
+
+        sums = [psum.tile([P, POOLED], F32, name=f"sum{t}") for t in range(OUT_BLOCKS)]
+        for k in range(BLOCKS):
+            largest = centres[k]
+            for d in range(NEIGHBOURS):
+                larger = held.tile([P, POOLED], F32, name=f"larger{k}_{d}")
+                looked_up = windows[k][:].indirect(offsets[:, d * PIECE:(d + 1) * PIECE])
+                nc.vector.tensor_tensor(larger[:], looked_up, largest[:], MAX)
+                largest = larger
+            pooled = held.tile([P, POOLED], BF16, name=f"pooled{k}")
+            nc.scalar.copy(pooled[:], largest[:])
+            for t in range(OUT_BLOCKS):
+                nc.tensor.matmul(sums[t][:], weights[:, k, t * P:(t + 1) * P], pooled[:],
+                                 start=(k == 0), stop=(k == BLOCKS - 1))
+
+        for t in range(OUT_BLOCKS):
+            result = held.tile([P, POOLED], F32, name=f"result{t}")
+            if t % 2 == 0:
+                nc.scalar.activation(result[:], sums[t][:], RELU, bias=bias[:, t:t + 1])
+            else:
+                nc.vector.tensor_scalar(result[:], sums[t][:], bias[:, t:t + 1], 0.0, ADD, MAX)
+            nc.sync.dma_start(out[t * P:(t + 1) * P, :], result[:])

@@ -35,23 +35,26 @@ def tile_lookup_pool_max_relu_kernel(tc, tab, x0, w, b, offs, out):
             nc.sync.dma_start(window[:], tab[rows, :])
             windows.append(window)
             centres.append(centre)
-            if k == 1:
-                nc.sync.dma_start(weights[:], w.rearrange("(k p) m -> p k m", p=P))
-                nc.sync.dma_start(bias[:], b.rearrange("(t p) one -> p (t one)", p=P))
+        nc.sync.dma_start(weights[:], w.rearrange("(k p) m -> p k m", p=P))
+        nc.sync.dma_start(bias[:], b.rearrange("(t p) one -> p (t one)", p=P))
 
         sums = [psum.tile([P, POOLED], F32, name=f"sum{t}") for t in range(OUT_BLOCKS)]
-        for k in range(BLOCKS):
-            largest = centres[k]
-            for d in range(NEIGHBOURS):
+        largest = list(centres)
+        for wave in range(BLOCKS + NEIGHBOURS - 1):
+            for k in range(BLOCKS):
+                d = wave - k
+                if not 0 <= d < NEIGHBOURS:
+                    continue
                 larger = held.tile([P, POOLED], F32, name=f"larger{k}_{d}")
                 looked_up = windows[k][:].indirect(offsets[:, d * PIECE:(d + 1) * PIECE])
-                nc.vector.tensor_tensor(larger[:], looked_up, largest[:], MAX)
-                largest = larger
-            pooled = held.tile([P, POOLED], BF16, name=f"pooled{k}")
-            nc.scalar.copy(pooled[:], largest[:])
-            for t in range(OUT_BLOCKS):
-                nc.tensor.matmul(sums[t][:], weights[:, k, t * P:(t + 1) * P], pooled[:],
-                                 start=(k == 0), stop=(k == BLOCKS - 1))
+                nc.vector.tensor_tensor(larger[:], looked_up, largest[k][:], MAX)
+                largest[k] = larger
+                if d == NEIGHBOURS - 1:
+                    pooled = held.tile([P, POOLED], BF16, name=f"pooled{k}")
+                    nc.scalar.copy(pooled[:], larger[:])
+                    for t in range(OUT_BLOCKS):
+                        nc.tensor.matmul(sums[t][:], weights[:, k, t * P:(t + 1) * P], pooled[:],
+                                         start=(k == 0), stop=(k == BLOCKS - 1))
 
         for t in range(OUT_BLOCKS):
             result = held.tile([P, POOLED], F32, name=f"result{t}")

@@ -6,6 +6,8 @@ NEIGHBOURS, POOLED = 3, 512
 OUT_ROWS = 512
 BLOCKS = ROWS // P
 OUT_BLOCKS = OUT_ROWS // P
+HALVES = (slice(0, POOLED // 2), slice(POOLED // 2, POOLED))
+BANK = 512
 PIECE = POOLED // 16
 
 F32, BF16, U16 = mybir.dt.float32, mybir.dt.bfloat16, mybir.dt.uint16
@@ -38,28 +40,38 @@ def tile_lookup_pool_max_relu_kernel(tc, tab, x0, w, b, offs, out):
         nc.sync.dma_start(weights[:], w.rearrange("(k p) m -> p k m", p=P))
         nc.sync.dma_start(bias[:], b.rearrange("(t p) one -> p (t one)", p=P))
 
-        sums = [psum.tile([P, POOLED], F32, name=f"sum{t}") for t in range(OUT_BLOCKS)]
+        sums = {(t, h): psum.tile([P, BANK], F32, name=f"sum{t}_{h}") for t in range(OUT_BLOCKS) for h in range(2)}
         largest = list(centres)
         for wave in range(BLOCKS + NEIGHBOURS - 1):
             for k in range(BLOCKS):
                 d = wave - k
                 if not 0 <= d < NEIGHBOURS:
                     continue
-                larger = held.tile([P, POOLED], F32, name=f"larger{k}_{d}")
+                if d == NEIGHBOURS - 1 and k < BLOCKS - 1:
+                    larger = centres[k + 1]
+                else:
+                    larger = held.tile([P, POOLED], F32, name=f"larger{k}_{d}")
                 looked_up = windows[k][:].indirect(offsets[:, d * PIECE:(d + 1) * PIECE])
                 nc.vector.tensor_tensor(larger[:], looked_up, largest[k][:], MAX)
                 largest[k] = larger
                 if d == NEIGHBOURS - 1:
                     pooled = held.tile([P, POOLED], BF16, name=f"pooled{k}")
-                    nc.scalar.copy(pooled[:], larger[:])
-                    for t in range(OUT_BLOCKS):
-                        nc.tensor.matmul(sums[t][:], weights[:, k, t * P:(t + 1) * P], pooled[:],
-                                         start=(k == 0), stop=(k == BLOCKS - 1))
+                    if k < BLOCKS - 1:
+                        nc.scalar.copy(pooled[:], larger[:])
+                    else:
+                        nc.vector.tensor_copy(pooled[:, HALVES[0]], larger[:, HALVES[0]])
+                        nc.scalar.copy(pooled[:, HALVES[1]], larger[:, HALVES[1]])
+                    for h, columns in enumerate(HALVES):
+                        for t in range(OUT_BLOCKS):
+                            nc.tensor.matmul(sums[t, h][:, :POOLED // 2], weights[:, k, t * P:(t + 1) * P],
+                                             pooled[:, columns], start=(k == 0), stop=(k == BLOCKS - 1))
 
-        for t in range(OUT_BLOCKS):
-            result = held.tile([P, POOLED], F32, name=f"result{t}")
-            if t % 2 == 0:
-                nc.scalar.activation(result[:], sums[t][:], RELU, bias=bias[:, t:t + 1])
-            else:
-                nc.vector.tensor_scalar(result[:], sums[t][:], bias[:, t:t + 1], 0.0, ADD, MAX)
-            nc.sync.dma_start(out[t * P:(t + 1) * P, :], result[:])
+        for h, columns in enumerate(HALVES):
+            for t in range(OUT_BLOCKS):
+                result = held.tile([P, POOLED // 2], F32, name=f"result{t}_{h}")
+                total = sums[t, h][:, :POOLED // 2]
+                if t % 2 == 0:
+                    nc.scalar.activation(result[:], total, RELU, bias=bias[:, t:t + 1])
+                else:
+                    nc.vector.tensor_scalar(result[:], total, bias[:, t:t + 1], 0.0, ADD, MAX)
+                nc.sync.dma_start(out[t * P:(t + 1) * P, columns], result[:])

@@ -61,17 +61,14 @@ def tile_lookup_pool_max_relu_kernel(tc, tab, x0, w, b, offs, out):
                     else:
                         nc.vector.tensor_copy(pooled[:, HALVES[0]], larger[:, HALVES[0]])
                         nc.scalar.copy(pooled[:, HALVES[1]], larger[:, HALVES[1]])
-                    for h, columns in enumerate(HALVES):
-                        for t in range(OUT_BLOCKS):
+                    for t in range(OUT_BLOCKS):
+                        for h, columns in enumerate(HALVES):
                             nc.tensor.matmul(sums[t, h][:, :POOLED // 2], weights[:, k, t * P:(t + 1) * P],
                                              pooled[:, columns], start=(k == 0), stop=(k == BLOCKS - 1))
 
-        for h, columns in enumerate(HALVES):
-            for t in range(OUT_BLOCKS):
-                result = held.tile([P, POOLED // 2], F32, name=f"result{t}_{h}")
-                total = sums[t, h][:, :POOLED // 2]
-                if t % 2 == 0:
-                    nc.scalar.activation(result[:], total, RELU, bias=bias[:, t:t + 1])
-                else:
-                    nc.vector.tensor_scalar(result[:], total, bias[:, t:t + 1], 0.0, ADD, MAX)
-                nc.sync.dma_start(out[t * P:(t + 1) * P, columns], result[:])
+        for t in range(OUT_BLOCKS):
+            result = held.tile([P, POOLED], F32, name=f"result{t}")
+            first, second = (sums[t, h][:, :POOLED // 2] for h in range(2))
+            nc.vector.tensor_scalar(result[:, HALVES[0]], first, bias[:, t:t + 1], 0.0, ADD, MAX)
+            nc.scalar.activation(result[:, HALVES[1]], second, RELU, bias=bias[:, t:t + 1])
+            nc.sync.dma_start(out[t * P:(t + 1) * P, :], result[:])

import concourse.mybir as mybir

P = 128
ROWS, TABLE_COLS = 512, 2048
NEIGHBOURS, POOLED = 3, 512
OUT_ROWS = 512
BLOCKS = ROWS // P
OUT_BLOCKS = OUT_ROWS // P
HALVES = (slice(0, POOLED // 2), slice(POOLED // 2, POOLED))
BANK = 512
PIECE = POOLED // 16

F32, BF16, U16 = mybir.dt.float32, mybir.dt.bfloat16, mybir.dt.uint16
ADD, MAX = mybir.AluOpType.add, mybir.AluOpType.max
RELU = mybir.ActivationFunctionType.Relu

FLOPS = 2 * ROWS * OUT_ROWS * POOLED


def tile_lookup_pool_max_relu_kernel(tc, tab, x0, w, b, offs, out):
    nc = tc.nc
    with (
        tc.tile_pool(name="held", bufs=1) as held,
        tc.psum_pool(name="psum", bufs=1) as psum,
    ):
        offsets = held.tile([P, NEIGHBOURS * PIECE], U16, name="offsets")
        nc.sync.dma_start(offsets[:], offs)

        windows, centres = [], []
        weights = held.tile([P, BLOCKS, OUT_ROWS], BF16, name="weights")
        bias = held.tile([P, OUT_BLOCKS], F32, name="bias")
        for k in range(BLOCKS):
            rows = slice(k * P, (k + 1) * P)
            window = held.tile([P, TABLE_COLS], F32, name=f"window{k}")
            centre = held.tile([P, POOLED], F32, name=f"centre{k}")
            nc.sync.dma_start(centre[:], x0[rows, :])
            nc.sync.dma_start(window[:], tab[rows, :])
            windows.append(window)
            centres.append(centre)
        nc.sync.dma_start(weights[:], w.rearrange("(k p) m -> p k m", p=P))
        nc.sync.dma_start(bias[:], b.rearrange("(t p) one -> p (t one)", p=P))

        sums = {(t, h): psum.tile([P, BANK], F32, name=f"sum{t}_{h}") for t in range(OUT_BLOCKS) for h in range(2)}
        largest = list(centres)
        for wave in range(BLOCKS + NEIGHBOURS - 1):
            for k in range(BLOCKS):
                d = wave - k
                if not 0 <= d < NEIGHBOURS:
                    continue
                if d == NEIGHBOURS - 1 and k < BLOCKS - 1:
                    larger = centres[k + 1]
                else:
                    larger = held.tile([P, POOLED], F32, name=f"larger{k}_{d}")
                looked_up = windows[k][:].indirect(offsets[:, d * PIECE:(d + 1) * PIECE])
                nc.vector.tensor_tensor(larger[:], looked_up, largest[k][:], MAX)
                largest[k] = larger
                if d == NEIGHBOURS - 1:
                    pooled = held.tile([P, POOLED], BF16, name=f"pooled{k}")
                    if k < BLOCKS - 1:
                        nc.scalar.copy(pooled[:], larger[:])
                    else:
                        nc.vector.tensor_copy(pooled[:, HALVES[0]], larger[:, HALVES[0]])
                        nc.scalar.copy(pooled[:, HALVES[1]], larger[:, HALVES[1]])
                    for t in range(OUT_BLOCKS):
                        for h, columns in enumerate(HALVES):
                            nc.tensor.matmul(sums[t, h][:, :POOLED // 2], weights[:, k, t * P:(t + 1) * P],
                                             pooled[:, columns], start=(k == 0), stop=(k == BLOCKS - 1))

        for t in range(OUT_BLOCKS):
            result = held.tile([P, POOLED], F32, name=f"result{t}")
            first, second = (sums[t, h][:, :POOLED // 2] for h in range(2))
            nc.vector.tensor_scalar(result[:, HALVES[0]], first, bias[:, t:t + 1], 0.0, ADD, MAX)
            nc.scalar.activation(result[:, HALVES[1]], second, RELU, bias=bias[:, t:t + 1])
            nc.sync.dma_start(out[t * P:(t + 1) * P, :], result[:])
